import numpy as np
import ml_dtypes


def mxq(x, axis, fmt="e4m3"):
    dtype, down = {"e4m3": (ml_dtypes.float8_e4m3fn, 7), "e5m2": (ml_dtypes.float8_e5m2, 14)}[fmt]
    v = np.moveaxis(np.asarray(x, np.float32).astype(ml_dtypes.bfloat16).astype(np.float64), axis, -1)
    blocks = v.reshape(v.shape[:-1] + (-1, 32))
    amax = np.abs(blocks).max(-1, keepdims=True)
    byte = np.maximum(np.where(amax > 0, np.frexp(amax)[1] - 1 + 127, 0) - down, 1)
    scale = np.exp2(byte - 127.0)
    codes = (blocks / scale).astype(np.float32).astype(dtype).astype(np.float64)
    return np.moveaxis((codes * scale).reshape(v.shape), -1, axis)


WIDE = False


def mx_kscale(k):
    if not WIDE:
        return np.ones(k)
    levels = np.array([10, -10, 5, -5, 0])
    if k % 512:
        return np.exp2(np.random.permutation(np.resize(levels, k // 32))).repeat(32)
    a = np.empty((k // 512, 16))
    for p in range(k // 512):
        a[p, :8] = np.random.permutation(np.resize(levels, 8))
        for g in range(8):
            far = levels[np.abs(levels - a[p, g]) >= 10]
            a[p, g + 8] = far[np.random.randint(len(far))]
    return np.exp2(a.ravel()).repeat(32)


def f64(x):
    return np.asarray(x).astype(np.float64)


def striped8(idx):
    return np.concatenate([v.reshape(-1, 16).T for v in idx]).astype(np.uint16)


def unstriped8(offs):
    return np.stack([offs[16 * g:16 * g + 16].T.reshape(-1) for g in range(8)]).astype(np.int64)


K, M, T, S = 512, 512, 1024, 512


def setup_inputs():
    n = np.random.standard_normal
    s = mx_kscale(K)[:, None]
    return {
        "xT": (n((K, T)) * s).astype(np.float32),
        "w": (n((K, M)) / np.sqrt(K) / s).astype(np.float32),
        "wgt": np.repeat(np.random.uniform(0.5, 2.0, (8, S)), 16, axis=0).astype(np.float32),
        "b": (0.3 * n(512)).astype(np.float32),
        "wgo": np.repeat(np.random.uniform(0.5, 2.0, (8, S)), 16, axis=0).astype(np.float32),
        "offs": striped8(np.stack([np.random.permutation(T)[:S] for _ in range(8)])),
        "offs2": striped8(np.stack([np.random.permutation(T)[:S] for _ in range(8)])),
    }


def reference(xT, w, wgt, b, wgo, offs, offs2):
    idx = unstriped8(offs)
    group = np.arange(K) % 512 // 64
    xg = f64(wgt)[np.arange(K) // 4 % 128] * f64(xT)[np.arange(K)[:, None], idx[group]]
    xT_ = mxq(xg, 0, "e4m3")
    w_ = mxq(f64(w), 0, "e4m3")
    y = w_.T @ xT_
    place = unstriped8(offs2)[np.arange(M) % 128 // 16]
    out = np.zeros((M, T))
    out[np.arange(M)[:, None], place] = f64(wgo)[np.arange(M) % 128] * (y + f64(b)[:, None])
    return out

@@ -1,0 +1,166 @@
+from contextlib import ExitStack
+
+import concourse.mybir as mybir
+
+K, M, T, S = 512, 512, 1024, 512
+P = 128
+PACK = 4
+HALF = S // 2
+M_TILES = M // P
+M_HALF = M // 2
+COLS = HALF // 16
+FLOPS = 2 * K * M * S
+
+F32 = mybir.dt.float32
+BF16 = mybir.dt.bfloat16
+U32 = mybir.dt.uint32
+U16 = mybir.dt.uint16
+U8 = mybir.dt.uint8
+FP8X4 = mybir.dt.float8_e4m3fn_x4
+MULT = mybir.AluOpType.mult
+IDENTITY = mybir.ActivationFunctionType.Identity
+
+
+def tile_list_hboth_bias_kernel(tc, xT, w, wgt, b, wgo, offs, offs2, out):
+    nc = tc.nc
+    x_rows = xT.rearrange("(p j) t -> p j t", j=PACK)
+    w_rows = w.rearrange("(p j) n -> p j n", j=PACK)
+    with ExitStack() as ctx:
+        keep = ctx.enter_context(tc.tile_pool(name="keep", bufs=1))
+        psum = ctx.enter_context(tc.psum_pool(name="psum", bufs=1))
+
+        offs_sb = keep.tile([P, S // 16], U16, name="offs_sb")
+        offs2_sb = keep.tile([P, S // 16], U16, name="offs2_sb")
+        b_sb = keep.tile([P, M_TILES], F32, name="b_sb")
+        warm = keep.tile([P, 1], F32, name="warm")
+        x_sb = [keep.tile([P, T], F32, name=f"x{j}") for j in range(PACK)]
+        wgt_sb = [keep.tile([P, HALF], F32, name=f"wgt{h}") for h in range(2)]
+        wgo_sb = [keep.tile([P, HALF], F32, name=f"wgo{h}") for h in range(2)]
+        w_raw = [keep.tile([P, PACK, M_HALF], F32, name=f"w_raw{u}") for u in range(2)]
+        w_grouped = [keep.tile([P, M_HALF, PACK], BF16, name=f"w_grouped{u}", align_bytes=64) for u in range(2)]
+        w_codes = [keep.tile([P, M_HALF], U32, name=f"w_codes{u}", align_bytes=64) for u in range(2)]
+        w_scales = [keep.tile([P, M_HALF], U8, name=f"w_scales{u}", align_bytes=64) for u in range(2)]
+        win = [keep.tile([P, T], F32, name=f"win{m}") for m in range(M_TILES)]
+        picked = [keep.tile([P, PACK, HALF], F32, name=f"picked{h}") for h in range(2)]
+        x_grouped = [keep.tile([P, HALF, PACK], BF16, name=f"x_grouped{h}", align_bytes=64) for h in range(2)]
+        x_codes = [keep.tile([P, HALF], U32, name=f"x_codes{h}", align_bytes=64) for h in range(2)]
+        x_scales = [keep.tile([P, HALF], U8, name=f"x_scales{h}", align_bytes=64) for h in range(2)]
+        y_sb = {}
+
+        def load_x(j):
+            nc.sync.dma_start(out=x_sb[j][:], in_=x_rows[:, j, :])
+
+        def load_w(u):
+            nc.sync.dma_start(out=w_raw[u][:], in_=w_rows[:, :, u * M_HALF : (u + 1) * M_HALF])
+
+        nc.sync.dma_start(offs_sb[:], offs)
+        nc.sync.dma_start(out=wgt_sb[0][:], in_=wgt[:, 0:HALF])
+        load_x(0)
+        load_x(1)
+        nc.sync.dma_start(out=wgt_sb[1][:], in_=wgt[:, HALF:S])
+        load_x(2)
+        load_x(3)
+        load_w(0)
+        nc.sync.dma_start(offs2_sb[:], offs2)
+        with nc.allow_non_contiguous_dma(reason="512 bias values onto the partitions"):
+            nc.sync.dma_start(out=b_sb[:], in_=b.rearrange("(m p) -> p m", p=P))
+        nc.sync.dma_start(out=wgo_sb[0][:], in_=wgo[:, 0:HALF])
+        load_w(1)
+        nc.sync.dma_start(out=wgo_sb[1][:], in_=wgo[:, HALF:S])
+
+        for m in range(M_TILES):
+            nc.vector.memset(win[m][:], 0.0)
+        nc.gpsimd.memset(warm[:], 0.0)
+        nc.scalar.activation(out=warm[:], in_=warm[:], func=IDENTITY)
+
+        def gather(j, h):
+            nc.vector.tensor_tensor(
+                picked[h][:, j, :],
+                x_sb[j][:].indirect(offs_sb[:, h * COLS : (h + 1) * COLS]),
+                wgt_sb[h][:],
+                MULT,
+            )
+
+        def group_pair(u, h):
+            nc.scalar.copy(
+                out=x_grouped[h][:, :, 2 * u : 2 * u + 2],
+                in_=picked[h][:, 2 * u : 2 * u + 2, :].rearrange("p j s -> p s j"),
+            )
+
+        def quantize_x(h):
+            nc.vector.quantize_mx(
+                out=x_codes[h][:].bitcast(FP8X4),
+                scales=x_scales[h][:],
+                in_=x_grouped[h][:].rearrange("p s j -> p (s j)"),
+            )
+
+        def quantize_w(u):
+            nc.vector.quantize_mx(
+                out=w_codes[u][:].bitcast(FP8X4),
+                scales=w_scales[u][:],
+                in_=w_grouped[u][:].rearrange("p n j -> p (n j)"),
+            )
+
+        def multiply(m, h):
+            acc = psum.tile([P, HALF], F32, name=f"acc{m}_{h}")
+            y_sb[m, h] = keep.tile([P, HALF], F32, name=f"y{m}_{h}")
+            u, cols = m // 2, slice(m % 2 * P, (m % 2 + 1) * P)
+            nc.tensor.matmul_mx(
+                out=acc[:],
+                lhsT=w_codes[u][:, cols].bitcast(FP8X4),
+                lhsT_scale=w_scales[u][:, cols],
+                rhs=x_codes[h][:].bitcast(FP8X4),
+                rhs_scale=x_scales[h][:],
+                start=True,
+                stop=True,
+            )
+            nc.scalar.activation(out=y_sb[m, h][:], in_=acc[:], func=IDENTITY, bias=b_sb[:, m : m + 1])
+
+        def scatter(m, h):
+            nc.vector.tensor_tensor(
+                win[m][:].indirect(offs2_sb[:, h * COLS : (h + 1) * COLS]),
+                y_sb[m, h][:],
+                wgo_sb[h][:],
+                MULT,
+            )
+
+        def store(m):
+            nc.sync.dma_start(out=out[m * P : (m + 1) * P, :], in_=win[m][:])
+
+        gather(0, 0)
+        gather(1, 0)
+        group_pair(0, 0)
+        gather(0, 1)
+        gather(2, 0)
+        gather(1, 1)
+        gather(3, 0)
+        group_pair(1, 0)
+        gather(2, 1)
+        group_pair(0, 1)
+        nc.vector.tensor_copy(out=w_grouped[0][:], in_=w_raw[0][:].rearrange("p j n -> p n j"))
+        quantize_x(0)
+        quantize_w(0)
+        multiply(0, 0)
+        gather(3, 1)
+        group_pair(1, 1)
+        multiply(1, 0)
+        scatter(0, 0)
+        quantize_x(1)
+        multiply(0, 1)
+        multiply(1, 1)
+        nc.scalar.copy(out=w_grouped[1][:], in_=w_raw[1][:].rearrange("p j n -> p n j"))
+        scatter(1, 0)
+        scatter(0, 1)
+        store(0)
+        quantize_w(1)
+        for m in (2, 3):
+            for h in range(2):
+                multiply(m, h)
+        scatter(1, 1)
+        store(1)
+        scatter(2, 0)
+        scatter(3, 0)
+        scatter(2, 1)
+        store(2)
+        scatter(3, 1)
+        store(3)

@@ -41,7 +41,8 @@ def tile_list_hboth_bias_kernel(tc, xT, w, wgt, b, wgo, offs, offs2, out):
         w_codes = [keep.tile([P, M_HALF], U32, name=f"w_codes{u}", align_bytes=64) for u in range(2)]
         w_scales = [keep.tile([P, M_HALF], U8, name=f"w_scales{u}", align_bytes=64) for u in range(2)]
         win = [keep.tile([P, T], F32, name=f"win{m}") for m in range(M_TILES)]
-        picked = [keep.tile([P, PACK, HALF], F32, name=f"picked{h}") for h in range(2)]
+        picked01 = [keep.tile([P, 2, HALF], F32, name=f"picked01_{h}") for h in range(2)]
+        picked23 = [keep.tile([P, 2, HALF], F32, name="picked23") for h in range(2)]
         x_grouped = [keep.tile([P, HALF, PACK], BF16, name=f"x_grouped{h}", align_bytes=64) for h in range(2)]
         x_codes = [keep.tile([P, HALF], U32, name=f"x_codes{h}", align_bytes=64) for h in range(2)]
         x_scales = [keep.tile([P, HALF], U8, name=f"x_scales{h}", align_bytes=64) for h in range(2)]
@@ -68,14 +69,14 @@ def tile_list_hboth_bias_kernel(tc, xT, w, wgt, b, wgo, offs, offs2, out):
         load_w(1)
         nc.sync.dma_start(out=wgo_sb[1][:], in_=wgo[:, HALF:S])
 
-        for m in range(M_TILES):
-            nc.vector.memset(win[m][:], 0.0)
         nc.gpsimd.memset(warm[:], 0.0)
+        for m in range(M_TILES):
+            (nc.vector if m < 2 else nc.gpsimd).memset(win[m][:], 0.0)
         nc.scalar.activation(out=warm[:], in_=warm[:], func=IDENTITY)
 
         def gather(j, h):
             nc.vector.tensor_tensor(
-                picked[h][:, j, :],
+                (picked01, picked23)[j // 2][h][:, j % 2, :],
                 x_sb[j][:].indirect(offs_sb[:, h * COLS : (h + 1) * COLS]),
                 wgt_sb[h][:],
                 MULT,
@@ -84,7 +85,7 @@ def tile_list_hboth_bias_kernel(tc, xT, w, wgt, b, wgo, offs, offs2, out):
         def group_pair(u, h):
             nc.scalar.copy(
                 out=x_grouped[h][:, :, 2 * u : 2 * u + 2],
-                in_=picked[h][:, 2 * u : 2 * u + 2, :].rearrange("p j s -> p s j"),
+                in_=(picked01, picked23)[u][h][:].rearrange("p j s -> p s j"),
             )
 
         def quantize_x(h):
@@ -94,12 +95,19 @@ def tile_list_hboth_bias_kernel(tc, xT, w, wgt, b, wgo, offs, offs2, out):
                 in_=x_grouped[h][:].rearrange("p s j -> p (s j)"),
             )
 
-        def quantize_w(u):
+        def quantize_w(u, cols=slice(0, M_HALF)):
             nc.vector.quantize_mx(
-                out=w_codes[u][:].bitcast(FP8X4),
-                scales=w_scales[u][:],
-                in_=w_grouped[u][:].rearrange("p n j -> p (n j)"),
+                out=w_codes[u][:, cols].bitcast(FP8X4),
+                scales=w_scales[u][:, cols],
+                in_=w_grouped[u][:, cols, :].rearrange("p n j -> p (n j)"),
             )
+
+        def group_w(copy, u, cols=slice(0, M_HALF)):
+            copy(out=w_grouped[u][:, cols, :], in_=w_raw[u][:, :, cols].rearrange("p j n -> p n j"))
+
+        lo, hi = slice(0, P), slice(P, 2 * P)
+
+        acc_of = {}
 
         def multiply(m, h):
             acc = psum.tile([P, HALF], F32, name=f"acc{m}_{h}")
@@ -114,7 +122,10 @@ def tile_list_hboth_bias_kernel(tc, xT, w, wgt, b, wgo, offs, offs2, out):
                 start=True,
                 stop=True,
             )
-            nc.scalar.activation(out=y_sb[m, h][:], in_=acc[:], func=IDENTITY, bias=b_sb[:, m : m + 1])
+            acc_of[m, h] = acc
+
+        def empty(m, h):
+            nc.scalar.activation(out=y_sb[m, h][:], in_=acc_of[m, h][:], func=IDENTITY, bias=b_sb[:, m : m + 1])
 
         def scatter(m, h):
             nc.vector.tensor_tensor(
@@ -135,27 +146,36 @@ def tile_list_hboth_bias_kernel(tc, xT, w, wgt, b, wgo, offs, offs2, out):
         gather(1, 1)
         gather(3, 0)
         group_pair(1, 0)
-        gather(2, 1)
-        group_pair(0, 1)
-        nc.vector.tensor_copy(out=w_grouped[0][:], in_=w_raw[0][:].rearrange("p j n -> p n j"))
+        group_w(nc.vector.tensor_copy, 0, lo)
         quantize_x(0)
-        quantize_w(0)
+        quantize_w(0, lo)
         multiply(0, 0)
+        group_w(nc.scalar.copy, 0, hi)
+        group_pair(0, 1)
+        gather(2, 1)
         gather(3, 1)
+        empty(0, 0)
         group_pair(1, 1)
+        quantize_w(0, hi)
         multiply(1, 0)
+        empty(1, 0)
         scatter(0, 0)
         quantize_x(1)
         multiply(0, 1)
         multiply(1, 1)
-        nc.scalar.copy(out=w_grouped[1][:], in_=w_raw[1][:].rearrange("p j n -> p n j"))
         scatter(1, 0)
+        group_w(nc.scalar.copy, 1)
+        quantize_w(1)
+        empty(0, 1)
         scatter(0, 1)
         store(0)
-        quantize_w(1)
+        empty(1, 1)
         for m in (2, 3):
-            for h in range(2):
-                multiply(m, h)
+            multiply(m, 0)
+            empty(m, 0)
+        for m in (2, 3):
+            multiply(m, 1)
+            empty(m, 1)
         scatter(1, 1)
         store(1)
         scatter(2, 0)

@@ -57,8 +57,8 @@ def tile_list_hboth_bias_kernel(tc, xT, w, wgt, b, wgo, offs, offs2, out):
         nc.sync.dma_start(offs_sb[:], offs)
         nc.sync.dma_start(out=wgt_sb[0][:], in_=wgt[:, 0:HALF])
         load_x(0)
-        load_x(1)
         nc.sync.dma_start(out=wgt_sb[1][:], in_=wgt[:, HALF:S])
+        load_x(1)
         load_x(2)
         load_x(3)
         load_w(0)
@@ -139,11 +139,11 @@ def tile_list_hboth_bias_kernel(tc, xT, w, wgt, b, wgo, offs, offs2, out):
             nc.sync.dma_start(out=out[m * P : (m + 1) * P, :], in_=win[m][:])
 
         gather(0, 0)
+        gather(0, 1)
         gather(1, 0)
         group_pair(0, 0)
-        gather(0, 1)
-        gather(2, 0)
         gather(1, 1)
+        gather(2, 0)
         gather(3, 0)
         group_pair(1, 0)
         group_w(nc.vector.tensor_copy, 0, lo)

@@ -1,6 +1,7 @@
 from contextlib import ExitStack
 
 import concourse.mybir as mybir
+from concourse.masks import make_identity
 
 K, M, T, S = 512, 512, 1024, 512
 P = 128
@@ -27,11 +28,14 @@ def tile_list_hboth_bias_kernel(tc, xT, w, wgt, b, wgo, offs, offs2, out):
     w_rows = w.rearrange("(p j) n -> p j n", j=PACK)
     with ExitStack() as ctx:
         keep = ctx.enter_context(tc.tile_pool(name="keep", bufs=1))
-        psum = ctx.enter_context(tc.psum_pool(name="psum", bufs=1))
+        psum = ctx.enter_context(tc.psum_pool(name="psum", bufs=7))
+        psum_b = ctx.enter_context(tc.psum_pool(name="psum_b", bufs=1))
 
         offs_sb = keep.tile([P, S // 16], U16, name="offs_sb")
         offs2_sb = keep.tile([P, S // 16], U16, name="offs2_sb")
         b_sb = keep.tile([P, M_TILES], F32, name="b_sb")
+        b_rows = keep.tile([P, P], F32, name="b_rows")
+        ident = keep.tile([P, P], F32, name="ident")
         warm = keep.tile([P, 1], F32, name="warm")
         x_sb = [keep.tile([P, T], F32, name=f"x{j}") for j in range(PACK)]
         wgt_sb = [keep.tile([P, HALF], F32, name=f"wgt{h}") for h in range(2)]
@@ -57,22 +61,26 @@ def tile_list_hboth_bias_kernel(tc, xT, w, wgt, b, wgo, offs, offs2, out):
         nc.sync.dma_start(offs_sb[:], offs)
         nc.sync.dma_start(out=wgt_sb[0][:], in_=wgt[:, 0:HALF])
         load_x(0)
+        nc.gpsimd.memset(b_rows[:], 0.0)
+        nc.sync.dma_start(out=b_rows[0:M_TILES, :], in_=b.rearrange("(m p) -> m p", p=P))
         nc.sync.dma_start(out=wgt_sb[1][:], in_=wgt[:, HALF:S])
         load_x(1)
         load_x(2)
         load_x(3)
         load_w(0)
         nc.sync.dma_start(offs2_sb[:], offs2)
-        with nc.allow_non_contiguous_dma(reason="512 bias values onto the partitions"):
-            nc.sync.dma_start(out=b_sb[:], in_=b.rearrange("(m p) -> p m", p=P))
         nc.sync.dma_start(out=wgo_sb[0][:], in_=wgo[:, 0:HALF])
         load_w(1)
         nc.sync.dma_start(out=wgo_sb[1][:], in_=wgo[:, HALF:S])
 
         nc.gpsimd.memset(warm[:], 0.0)
+        make_identity(nc, ident[:])
         for m in range(M_TILES):
             (nc.vector if m < 2 else nc.gpsimd).memset(win[m][:], 0.0)
         nc.scalar.activation(out=warm[:], in_=warm[:], func=IDENTITY)
+        b_columns = psum_b.tile([P, P], F32, name="b_columns")
+        nc.tensor.transpose(b_columns[:], b_rows[:], ident[:])
+        nc.scalar.copy(out=b_sb[:], in_=b_columns[:, 0:M_TILES])
 
         def gather(j, h):
             nc.vector.tensor_tensor(
@@ -110,7 +118,7 @@ def tile_list_hboth_bias_kernel(tc, xT, w, wgt, b, wgo, offs, offs2, out):
         acc_of = {}
 
         def multiply(m, h):
-            acc = psum.tile([P, HALF], F32, name=f"acc{m}_{h}")
+            acc = psum.tile([P, HALF], F32, name="acc")
             y_sb[m, h] = keep.tile([P, HALF], F32, name=f"y{m}_{h}")
             u, cols = m // 2, slice(m % 2 * P, (m % 2 + 1) * P)
             nc.tensor.matmul_mx(

@@ -76,7 +76,7 @@ def tile_list_hboth_bias_kernel(tc, xT, w, wgt, b, wgo, offs, offs2, out):
         nc.gpsimd.memset(warm[:], 0.0)
         make_identity(nc, ident[:])
         for m in range(M_TILES):
-            (nc.vector if m < 2 else nc.gpsimd).memset(win[m][:], 0.0)
+            (nc.vector if m < 3 else nc.gpsimd).memset(win[m][:], 0.0)
         nc.scalar.activation(out=warm[:], in_=warm[:], func=IDENTITY)
         b_columns = psum_b.tile([P, P], F32, name="b_columns")
         nc.tensor.transpose(b_columns[:], b_rows[:], ident[:])

from contextlib import ExitStack

import concourse.mybir as mybir
from concourse.masks import make_identity

K, M, T, S = 512, 512, 1024, 512
P = 128
PACK = 4
HALF = S // 2
M_TILES = M // P
M_HALF = M // 2
COLS = HALF // 16
FLOPS = 2 * K * M * S

F32 = mybir.dt.float32
BF16 = mybir.dt.bfloat16
U32 = mybir.dt.uint32
U16 = mybir.dt.uint16
U8 = mybir.dt.uint8
FP8X4 = mybir.dt.float8_e4m3fn_x4
MULT = mybir.AluOpType.mult
IDENTITY = mybir.ActivationFunctionType.Identity


def tile_list_hboth_bias_kernel(tc, xT, w, wgt, b, wgo, offs, offs2, out):
    nc = tc.nc
    x_rows = xT.rearrange("(p j) t -> p j t", j=PACK)
    w_rows = w.rearrange("(p j) n -> p j n", j=PACK)
    with ExitStack() as ctx:
        keep = ctx.enter_context(tc.tile_pool(name="keep", bufs=1))
        psum = ctx.enter_context(tc.psum_pool(name="psum", bufs=7))
        psum_b = ctx.enter_context(tc.psum_pool(name="psum_b", bufs=1))

        offs_sb = keep.tile([P, S // 16], U16, name="offs_sb")
        offs2_sb = keep.tile([P, S // 16], U16, name="offs2_sb")
        b_sb = keep.tile([P, M_TILES], F32, name="b_sb")
        b_rows = keep.tile([P, P], F32, name="b_rows")
        ident = keep.tile([P, P], F32, name="ident")
        warm = keep.tile([P, 1], F32, name="warm")
        x_sb = [keep.tile([P, T], F32, name=f"x{j}") for j in range(PACK)]
        wgt_sb = [keep.tile([P, HALF], F32, name=f"wgt{h}") for h in range(2)]
        wgo_sb = [keep.tile([P, HALF], F32, name=f"wgo{h}") for h in range(2)]
        w_raw = [keep.tile([P, PACK, M_HALF], F32, name=f"w_raw{u}") for u in range(2)]
        w_grouped = [keep.tile([P, M_HALF, PACK], BF16, name=f"w_grouped{u}", align_bytes=64) for u in range(2)]
        w_codes = [keep.tile([P, M_HALF], U32, name=f"w_codes{u}", align_bytes=64) for u in range(2)]
        w_scales = [keep.tile([P, M_HALF], U8, name=f"w_scales{u}", align_bytes=64) for u in range(2)]
        win = [keep.tile([P, T], F32, name=f"win{m}") for m in range(M_TILES)]
        picked01 = [keep.tile([P, 2, HALF], F32, name=f"picked01_{h}") for h in range(2)]
        picked23 = [keep.tile([P, 2, HALF], F32, name="picked23") for h in range(2)]
        x_grouped = [keep.tile([P, HALF, PACK], BF16, name=f"x_grouped{h}", align_bytes=64) for h in range(2)]
        x_codes = [keep.tile([P, HALF], U32, name=f"x_codes{h}", align_bytes=64) for h in range(2)]
        x_scales = [keep.tile([P, HALF], U8, name=f"x_scales{h}", align_bytes=64) for h in range(2)]
        y_sb = {}

        def load_x(j):
            nc.sync.dma_start(out=x_sb[j][:], in_=x_rows[:, j, :])

        def load_w(u):
            nc.sync.dma_start(out=w_raw[u][:], in_=w_rows[:, :, u * M_HALF : (u + 1) * M_HALF])

        nc.sync.dma_start(offs_sb[:], offs)
        nc.sync.dma_start(out=wgt_sb[0][:], in_=wgt[:, 0:HALF])
        load_x(0)
        nc.gpsimd.memset(b_rows[:], 0.0)
        nc.sync.dma_start(out=b_rows[0:M_TILES, :], in_=b.rearrange("(m p) -> m p", p=P))
        nc.sync.dma_start(out=wgt_sb[1][:], in_=wgt[:, HALF:S])
        load_x(1)
        load_x(2)
        load_x(3)
        load_w(0)
        nc.sync.dma_start(offs2_sb[:], offs2)
        nc.sync.dma_start(out=wgo_sb[0][:], in_=wgo[:, 0:HALF])
        load_w(1)
        nc.sync.dma_start(out=wgo_sb[1][:], in_=wgo[:, HALF:S])

        nc.gpsimd.memset(warm[:], 0.0)
        make_identity(nc, ident[:])
        for m in range(M_TILES):
            (nc.vector if m < 3 else nc.gpsimd).memset(win[m][:], 0.0)
        nc.scalar.activation(out=warm[:], in_=warm[:], func=IDENTITY)
        b_columns = psum_b.tile([P, P], F32, name="b_columns")
        nc.tensor.transpose(b_columns[:], b_rows[:], ident[:])
        nc.scalar.copy(out=b_sb[:], in_=b_columns[:, 0:M_TILES])

        def gather(j, h):
            nc.vector.tensor_tensor(
                (picked01, picked23)[j // 2][h][:, j % 2, :],
                x_sb[j][:].indirect(offs_sb[:, h * COLS : (h + 1) * COLS]),
                wgt_sb[h][:],
                MULT,
            )

        def group_pair(u, h):
            nc.scalar.copy(
                out=x_grouped[h][:, :, 2 * u : 2 * u + 2],
                in_=(picked01, picked23)[u][h][:].rearrange("p j s -> p s j"),
            )

        def quantize_x(h):
            nc.vector.quantize_mx(
                out=x_codes[h][:].bitcast(FP8X4),
                scales=x_scales[h][:],
                in_=x_grouped[h][:].rearrange("p s j -> p (s j)"),
            )

        def quantize_w(u, cols=slice(0, M_HALF)):
            nc.vector.quantize_mx(
                out=w_codes[u][:, cols].bitcast(FP8X4),
                scales=w_scales[u][:, cols],
                in_=w_grouped[u][:, cols, :].rearrange("p n j -> p (n j)"),
            )

        def group_w(copy, u, cols=slice(0, M_HALF)):
            copy(out=w_grouped[u][:, cols, :], in_=w_raw[u][:, :, cols].rearrange("p j n -> p n j"))

        lo, hi = slice(0, P), slice(P, 2 * P)

        acc_of = {}

        def multiply(m, h):
            acc = psum.tile([P, HALF], F32, name="acc")
            y_sb[m, h] = keep.tile([P, HALF], F32, name=f"y{m}_{h}")
            u, cols = m // 2, slice(m % 2 * P, (m % 2 + 1) * P)
            nc.tensor.matmul_mx(
                out=acc[:],
                lhsT=w_codes[u][:, cols].bitcast(FP8X4),
                lhsT_scale=w_scales[u][:, cols],
                rhs=x_codes[h][:].bitcast(FP8X4),
                rhs_scale=x_scales[h][:],
                start=True,
                stop=True,
            )
            acc_of[m, h] = acc

        def empty(m, h):
            nc.scalar.activation(out=y_sb[m, h][:], in_=acc_of[m, h][:], func=IDENTITY, bias=b_sb[:, m : m + 1])

        def scatter(m, h):
            nc.vector.tensor_tensor(
                win[m][:].indirect(offs2_sb[:, h * COLS : (h + 1) * COLS]),
                y_sb[m, h][:],
                wgo_sb[h][:],
                MULT,
            )

        def store(m):
            nc.sync.dma_start(out=out[m * P : (m + 1) * P, :], in_=win[m][:])

        gather(0, 0)
        gather(0, 1)
        gather(1, 0)
        group_pair(0, 0)
        gather(1, 1)
        gather(2, 0)
        gather(3, 0)
        group_pair(1, 0)
        group_w(nc.vector.tensor_copy, 0, lo)
        quantize_x(0)
        quantize_w(0, lo)
        multiply(0, 0)
        group_w(nc.scalar.copy, 0, hi)
        group_pair(0, 1)
        gather(2, 1)
        gather(3, 1)
        empty(0, 0)
        group_pair(1, 1)
        quantize_w(0, hi)
        multiply(1, 0)
        empty(1, 0)
        scatter(0, 0)
        quantize_x(1)
        multiply(0, 1)
        multiply(1, 1)
        scatter(1, 0)
        group_w(nc.scalar.copy, 1)
        quantize_w(1)
        empty(0, 1)
        scatter(0, 1)
        store(0)
        empty(1, 1)
        for m in (2, 3):
            multiply(m, 0)
            empty(m, 0)
        for m in (2, 3):
            multiply(m, 1)
            empty(m, 1)
        scatter(1, 1)
        store(1)
        scatter(2, 0)
        scatter(3, 0)
        scatter(2, 1)
        store(2)
        scatter(3, 1)
        store(3)
